import numpy as np
import ml_dtypes


def mxq(x, axis, fmt="e4m3"):
    dtype, down = {"e4m3": (ml_dtypes.float8_e4m3fn, 7), "e5m2": (ml_dtypes.float8_e5m2, 14)}[fmt]
    v = np.moveaxis(np.asarray(x, np.float32).astype(ml_dtypes.bfloat16).astype(np.float64), axis, -1)
    blocks = v.reshape(v.shape[:-1] + (-1, 32))
    amax = np.abs(blocks).max(-1, keepdims=True)
    byte = np.maximum(np.where(amax > 0, np.frexp(amax)[1] - 1 + 127, 0) - down, 1)
    scale = np.exp2(byte - 127.0)
    codes = (blocks / scale).astype(np.float32).astype(dtype).astype(np.float64)
    return np.moveaxis((codes * scale).reshape(v.shape), -1, axis)


WIDE = False


def mx_kscale(k):
    if not WIDE:
        return np.ones(k)
    levels = np.array([10, -10, 5, -5, 0])
    if k % 512:
        return np.exp2(np.random.permutation(np.resize(levels, k // 32))).repeat(32)
    a = np.empty((k // 512, 16))
    for p in range(k // 512):
        a[p, :8] = np.random.permutation(np.resize(levels, 8))
        for g in range(8):
            far = levels[np.abs(levels - a[p, g]) >= 10]
            a[p, g + 8] = far[np.random.randint(len(far))]
    return np.exp2(a.ravel()).repeat(32)


def f64(x):
    return np.asarray(x).astype(np.float64)


def striped(idx):
    return np.tile(idx.reshape(-1, 16).T, (8, 1)).astype(np.uint16)


def unstriped(offs):
    return offs[:16].T.reshape(-1).astype(np.int64)


E2M1 = np.array([0.0, 0.5, 1.0, 1.5, 2.0, 3.0, 4.0, 6.0, -0.0, -0.5, -1.0, -1.5, -2.0, -3.0, -4.0, -6.0])


def pack_weight(w, fmt):
    k, n = w.shape
    w = f64(np.asarray(w, np.float32).astype(ml_dtypes.bfloat16)).reshape(k // 32, 32, n)
    amax = np.abs(w).max(1)
    if fmt == "e4m3":
        byte = np.frexp(amax)[1] - 1 + 127 - 7
    else:
        mant, ex = np.frexp(amax / 6.0)
        byte = np.where(mant > 0.5, ex, ex - 1) + 127
    byte = np.clip(np.where(amax > 0, byte, 1), 1, 254)
    scaled = (w * np.exp2(127.0 - byte)[:, None, :]).reshape(k, n).astype(np.float32)
    by_word = np.ascontiguousarray(scaled.reshape(k // 512, 128, 4, n).transpose(0, 1, 3, 2))
    if fmt == "e4m3":
        words = by_word.astype(ml_dtypes.float8_e4m3fn).view(np.uint8)
    else:
        c = by_word.astype(ml_dtypes.float4_e2m1fn).view(np.uint8) & 0xF
        words = (c[..., 0::2] | (c[..., 1::2] << 4)).reshape(k // 512, 128, 2 * n)
    return np.ascontiguousarray(words), np.ascontiguousarray(byte.astype(np.uint8).reshape(k // 512, 16, n))


def unpack_weight(words, scales, fmt):
    g, _, n = scales.shape
    words = np.ascontiguousarray(words).reshape(g, 128, n, -1)
    if fmt == "e4m3":
        vals = words.view(ml_dtypes.float8_e4m3fn).astype(np.float64)
    else:
        nib = np.empty((g, 128, n, 4), np.uint8)
        nib[..., 0::2] = words & 0xF
        nib[..., 1::2] = words >> 4
        vals = E2M1[nib]
    vals = vals * np.repeat(np.exp2(scales.astype(np.float64) - 127.0), 8, axis=1)[..., None]
    return vals.transpose(0, 1, 3, 2).reshape(g * 512, n)


def gelu(v):
    return 0.5 * v * (1.0 + np.tanh(np.sqrt(2.0 / np.pi) * (v + 0.044715 * v**3)))


K, T, S, H, T3, S2, P = 1024, 4096, 1024, 512, 2048, 512, 512


def setup_inputs():
    n = np.random.standard_normal
    s = mx_kscale(K)[:, None]
    u = mx_kscale(H)[:, None]
    d = {}
    d["tab_words"], d["tab_scales"] = pack_weight(n((K, T)) * s, "e4m3")
    d["offs"] = striped(np.random.permutation(T)[:S])
    d["w1"] = (1.5 * n((K, H)) / s / K ** 0.5).astype(np.float32)
    d["w2_words"], d["w2_scales"] = pack_weight(n((K, H)) / s / K ** 0.5, "e4m3")
    d["w3_words"], d["w3_scales"] = pack_weight(1.5 * n((K, H)) / s * u.T / K ** 0.5, "e2m1")
    d["tab2_words"], d["tab2_scales"] = pack_weight(n((H, T3)) / u / H ** 0.5, "e4m3")
    d["offs2"] = striped(np.random.permutation(T3)[:S2])
    d["pos1"] = striped(np.random.permutation(S)[:P])
    d["pos2"] = striped(np.random.permutation(S)[:P])
    d["rel"] = (1.3 * np.exp(0.4 * n((S2, P)))).astype(np.float32)
    return d


def reference(tab_words, tab_scales, offs, w1, w2_words, w2_scales, w3_words, w3_scales,
              tab2_words, tab2_scales, offs2, pos1, pos2, rel):
    v = unpack_weight(tab_words, tab_scales, "e4m3")[:, unstriped(offs)]
    w2 = unpack_weight(w2_words, w2_scales, "e4m3")
    w3 = unpack_weight(w3_words, w3_scales, "e2m1")
    inner = np.tanh(mxq(f64(w1), 0, "e4m3").T @ v)
    shape = np.tanh(inner + (w2.T @ v))
    h = shape * (w3.T @ v)
    v2 = unpack_weight(tab2_words, tab2_scales, "e4m3")[:, unstriped(offs2)]
    e = v2.T @ mxq(h, 0, "e4m3")
    return e[:, unstriped(pos1)] - np.tanh(f64(rel) * e[:, unstriped(pos2)])

@@ -1,0 +1,262 @@
+from contextlib import ExitStack
+
+import concourse.mybir as mybir
+
+K, T, S, H, T3, S2, NP = 1024, 4096, 1024, 512, 2048, 512, 512
+FLOPS = 2 * (3 * K * H * S + H * S2 * S)
+
+F32 = mybir.dt.float32
+BF16 = mybir.dt.bfloat16
+I32 = mybir.dt.int32
+U32 = mybir.dt.uint32
+U16 = mybir.dt.uint16
+U8 = mybir.dt.uint8
+FP8X4 = mybir.dt.float8_e4m3fn_x4
+FP4X4 = mybir.dt.float4_e2m1fn_x4
+TANH = mybir.ActivationFunctionType.Tanh
+ADD = mybir.AluOpType.add
+MULT = mybir.AluOpType.mult
+SUB = mybir.AluOpType.subtract
+
+P = 128
+PACK = 4
+PASSES = K // (P * PACK)
+UNIT = 128
+UNITS = S // UNIT
+BANK = 512
+PER_COLUMN = 16
+M_TILES = S2 // P
+
+
+def tile_list_impulse_template_scores_kernel(
+    tc, tab_words, tab_scales, offs, w1, w2_words, w2_scales, w3_words, w3_scales,
+    tab2_words, tab2_scales, offs2, pos1, pos2, rel, out,
+):
+    nc = tc.nc
+    with ExitStack() as ctx:
+        keep = ctx.enter_context(tc.tile_pool(name="keep", bufs=1))
+        reused = ctx.enter_context(tc.tile_pool(name="reused", bufs=1))
+        ring = ctx.enter_context(tc.tile_pool(name="ring", bufs=3))
+        psum = ctx.enter_context(tc.psum_pool(name="psum", bufs=1))
+
+        def held(shape, dtype, name):
+            return keep.tile(shape, dtype, name=name, align_bytes=64)
+
+        def placed(shape, dtype, name, offset):
+            return reused.tile(shape, dtype, name=name, align_bytes=64, offset=offset)
+
+        idx = held([P, S // PER_COLUMN], U16, "idx")
+        idx2 = held([P, S2 // PER_COLUMN], U16, "idx2")
+        p1 = held([P, NP // PER_COLUMN], U16, "p1")
+        p2 = held([P, NP // PER_COLUMN], U16, "p2")
+
+        tab_scale_rows = placed([P, T], U8, "tab_scale_rows", 0)
+        w_scale_rows = placed([P, PASSES, H], U8, "w_scale_rows", 8192 - 512)
+        v_scales_pass1 = held([P, S], U8, "v_scales_pass1")
+        tab2_scale_rows = held([P, T3], U8, "tab2_scale_rows")
+        for plane in (tab_scale_rows, w_scale_rows, v_scales_pass1, tab2_scale_rows):
+            nc.vector.memset(plane[:].bitcast(I32), 0)
+
+        nc.sync.dma_start(idx[:], offs)
+        for q in range(4):
+            nc.gpsimd.dma_start(
+                tab_scale_rows[32 * q : 32 * q + 8, :].bitcast(I32),
+                tab_scales[:, 4 * q : 4 * q + 4, :].bitcast(I32),
+            )
+        w1_raw = [held([P, PACK, H], F32, "w1_raw%d" % a) for a in range(PASSES)]
+        for a in range(PASSES):
+            nc.sync.dma_start(w1_raw[a][:], w1[512 * a : 512 * (a + 1), :].rearrange("(p j) c -> p j c", j=PACK))
+        w3_raw = held([P, PASSES, 2 * H], U8, "w3_raw")
+        nc.sync.dma_start(w3_raw[:].bitcast(I32), w3_words.rearrange("a p b -> p a b").bitcast(I32))
+        for first_row, scales in ((0, w3_scales), (4, w2_scales)):
+            for q in range(4):
+                nc.gpsimd.dma_start(
+                    w_scale_rows[32 * q + first_row : 32 * q + first_row + 4].bitcast(I32),
+                    scales[:, 4 * q : 4 * q + 4, :].rearrange("a r n -> r a n").bitcast(I32),
+                )
+        tab = [placed([P, T], U32, "tab%d" % a, 12288 + 16384 * a) for a in range(PASSES)]
+        for a in range(PASSES):
+            nc.sync.dma_start(tab[a][:].bitcast(I32), tab_words[a].rearrange("p t i -> p (t i)").bitcast(I32))
+        w2_raw = held([P, PASSES, H], U32, "w2_raw")
+        nc.sync.dma_start(w2_raw[:].bitcast(I32), w2_words.rearrange("a p c i -> p a (c i)").bitcast(I32))
+        for q in range(4):
+            nc.sync.dma_start(
+                tab2_scale_rows[32 * q : 32 * q + 4, :].bitcast(I32),
+                tab2_scales[0, 4 * q : 4 * q + 4, :].bitcast(I32),
+            )
+        tab2 = held([P, T3], U32, "tab2")
+        nc.sync.dma_start(tab2[:].bitcast(I32), tab2_words[0].rearrange("p t i -> p (t i)").bitcast(I32))
+        nc.sync.dma_start(idx2[:], offs2)
+        rel_rows = held([P, M_TILES, NP], F32, "rel_rows")
+        nc.sync.dma_start(rel_rows[:], rel.rearrange("(m p) n -> p m n", p=P))
+        nc.sync.dma_start(p2[:], pos2)
+        nc.sync.dma_start(p1[:], pos1)
+
+        def entries(lst, first, count):
+            return lst[:, first // PER_COLUMN : (first + count) // PER_COLUMN]
+
+        v_scales = held([P, S], U8, "v_scales")
+        nc.vector.tensor_copy(v_scales[:], tab_scale_rows[:].indirect(idx[:]))
+        nc.gpsimd.dma_start(v_scales_pass1[0:100, :].bitcast(I32), v_scales[4:104, :].bitcast(I32))
+
+        w1_codes = [held([P, H], U32, "w1_codes%d" % a) for a in range(PASSES)]
+        w1_planes = [placed([P, H], U8, "w1_planes%d" % a, H * a) for a in range(PASSES)]
+        w3_codes = placed([P, PASSES, 2 * H], U8, "w3_codes", 2048)
+        for a in range(PASSES):
+            grouped = held([P, H * PACK], BF16, "w1_grouped%d" % a)
+            nc.scalar.copy(
+                grouped[:].rearrange("p (t m j) -> p m t j", t=PACK, j=PACK),
+                w1_raw[a][:].rearrange("p j (m t) -> p m t j", t=PACK),
+            )
+            nc.vector.quantize_mx(out=w1_codes[a][:].bitcast(FP8X4), scales=w1_planes[a][:], in_=grouped[:])
+            nc.vector.tensor_copy(
+                w3_codes[:, a, :].rearrange("p (t m b) -> p t m b", t=PACK, b=2),
+                w3_raw[:, a, :].rearrange("p (m t b) -> p t m b", t=PACK, b=2),
+            )
+        w_planes = placed([P, PASSES, H], U8, "w_planes", 1024)
+        nc.vector.tensor_copy(
+            w_planes[:].rearrange("p a (t m) -> p a t m", t=PACK),
+            w_scale_rows[:].rearrange("p a (m t) -> p a t m", t=PACK),
+        )
+
+        v_words = [placed([P, PASSES * BANK], U32, "v_words%d" % half, 4096 + 4096 * half) for half in range(2)]
+        for a in range(PASSES):
+            for half in range(2):
+                nc.vector.tensor_copy(
+                    v_words[half][:, a * BANK : (a + 1) * BANK], tab[a][:].indirect(entries(idx, half * BANK, BANK))
+                )
+        w2_codes = placed([P, PASSES, H], U32, "w2_codes", 12288)
+        nc.vector.tensor_copy(
+            w2_codes[:].rearrange("p a (t m) -> p a t m", t=PACK),
+            w2_raw[:].rearrange("p a (m t) -> p a t m", t=PACK),
+        )
+
+        def one_pass(bank, a, unit, stationary, moving_planes):
+            cols = slice(unit * UNIT, (unit + 1) * UNIT)
+            half, first = divmod(unit * UNIT, BANK)
+            for t in range(PACK):
+                codes, plane = stationary(a, t)
+                nc.tensor.matmul_mx(
+                    out=bank[:, t, :],
+                    lhsT=codes,
+                    lhsT_scale=plane,
+                    rhs=v_words[half][:, a * BANK + first : a * BANK + first + UNIT].bitcast(FP8X4),
+                    rhs_scale=moving_planes[a][:, cols],
+                    start=(a == 0 and t == 0),
+                    stop=(a == PASSES - 1 and t == PACK - 1),
+                )
+
+        opened = {}
+
+        def begin(tag, bufs, unit, stationary, moving_planes):
+            bank = psum.tile([P, PACK, UNIT], F32, name=tag, tag=tag, bufs=bufs)
+            one_pass(bank, 0, unit, stationary, moving_planes)
+            opened[tag, unit] = bank
+
+        def product(tag, bufs, unit, stationary, moving_planes):
+            if (tag, unit) not in opened:
+                begin(tag, bufs, unit, stationary, moving_planes)
+            bank = opened[tag, unit]
+            one_pass(bank, 1, unit, stationary, moving_planes)
+            return bank[:].rearrange("p t j -> p j t")
+
+        def w1_tile(a, t):
+            return w1_codes[a][:, P * t : P * (t + 1)].bitcast(FP8X4), w1_planes[a][:, P * t : P * (t + 1)]
+
+        def w2_tile(a, t):
+            return w2_codes[:, a, P * t : P * (t + 1)].bitcast(FP8X4), w_planes[4:P, a, P * t : P * (t + 1)]
+
+        def w3_tile(a, t):
+            return w3_codes[:, a, 2 * P * t : 2 * P * (t + 1)].bitcast(FP4X4), w_planes[:, a, P * t : P * (t + 1)]
+
+        packed_planes = (v_scales[:], v_scales[4:P, :])
+        apart_planes = (v_scales[:], v_scales_pass1[:])
+
+        h_codes = held([P, S], U32, "h_codes")
+        h_plane = held([P, S], U8, "h_plane")
+        v2_words = {}
+        v2_plane = {}
+        scores = [held([P, S], F32, "scores%d" % m) for m in range(M_TILES)]
+
+        def gather_templates(half):
+            v2_plane[half] = placed([P, 256], U8, "v2_plane%d" % half, 4096 + 4096 * half + 1024)
+            v2_words[half] = placed([P, 256], U32, "v2_words%d" % half, 4096 + 4096 * half)
+            nc.vector.tensor_copy(v2_plane[half][:], tab2_scale_rows[:].indirect(entries(idx2, 256 * half, 256)))
+            nc.vector.tensor_copy(v2_words[half][:], tab2[:].indirect(entries(idx2, 256 * half, 256)))
+
+        def score(m, first, widths):
+            bank = psum.tile([P, BANK], F32, name="z1", tag="z1", bufs=3)
+            rows = slice(P * (m % 2), P * (m % 2 + 1))
+            at = 0
+            for width in widths:
+                cols = slice(first + at, first + at + width)
+                nc.tensor.matmul_mx(
+                    out=bank[:, at : at + width],
+                    lhsT=v2_words[m // 2][:, rows].bitcast(FP8X4),
+                    lhsT_scale=v2_plane[m // 2][:, rows],
+                    rhs=h_codes[:, cols].bitcast(FP8X4),
+                    rhs_scale=h_plane[:, cols],
+                    start=True,
+                    stop=True,
+                )
+                at = at + width
+            nc.scalar.copy(scores[m][:, first : first + at], bank[:, 0:at])
+
+        def interleaved(tile):
+            return tile[:].rearrange("p (j t) -> p j t", t=PACK)
+
+        for unit in range(3):
+            begin("z1", 3, unit, w1_tile, packed_planes)
+        for unit in range(3):
+            begin("z3", 3, unit, w3_tile, apart_planes)
+        shapes = {}
+        for step in range(UNITS + 1):
+            if step < UNITS:
+                z1 = product("z1", 3, step, w1_tile, packed_planes)
+                z2 = product("z2", 2, step, w2_tile, packed_planes)
+                inner = ring.tile([P, BANK], F32, name="inner")
+                nc.scalar.activation(interleaved(inner), z1, TANH)
+            if step >= 1:
+                z3 = product("z3", 3, step - 1, w3_tile, apart_planes)
+                h = ring.tile([P, BANK], BF16, name="h", align_bytes=64)
+                nc.vector.tensor_tensor(interleaved(h), z3, interleaved(shapes[step - 1]), MULT)
+            if step < UNITS:
+                total = ring.tile([P, BANK], F32, name="total")
+                nc.vector.tensor_tensor(interleaved(total), z2, interleaved(inner), ADD)
+                shape = ring.tile([P, BANK], F32, name="shape")
+                nc.scalar.activation(shape[:], total[:], TANH)
+                shapes[step] = shape
+            if step >= 1:
+                cols = slice((step - 1) * UNIT, step * UNIT)
+                nc.vector.quantize_mx(out=h_codes[:, cols].bitcast(FP8X4), scales=h_plane[:, cols], in_=h[:])
+            if step == 4:
+                gather_templates(0)
+            if step == 5:
+                score(0, 0, [BANK])
+                score(1, 0, [BANK])
+            if step == 7:
+                score(0, BANK, [256, 128])
+        score(0, S - UNIT, [UNIT])
+        gather_templates(1)
+        score(1, BANK, [BANK])
+
+        def bounded(m):
+            scaled = ring.tile([P, NP], F32, name="scaled")
+            nc.vector.tensor_tensor(scaled[:], scores[m][:].indirect(p2[:]), rel_rows[:, m, :], MULT)
+            bound = ring.tile([P, NP], F32, name="bound")
+            nc.scalar.activation(bound[:], scaled[:], TANH)
+            return bound
+
+        def finish(m, bound):
+            result = ring.tile([P, NP], F32, name="result")
+            nc.vector.tensor_tensor(result[:], scores[m][:].indirect(p1[:]), bound[:], SUB)
+            nc.sync.dma_start(out[P * m : P * (m + 1), :], result[:])
+
+        bounds = {0: bounded(0)}
+        for m in range(M_TILES):
+            if m + 1 < M_TILES:
+                bounds[m + 1] = bounded(m + 1)
+            if m + 2 < M_TILES:
+                score(m + 2, 0, [BANK])
+                score(m + 2, BANK, [BANK])
+            finish(m, bounds[m])

@@ -22,7 +22,8 @@ P = 128
 PACK = 4
 PASSES = K // (P * PACK)
 UNIT = 128
-UNITS = S // UNIT
+WIDE = 256
+STEPS = S // WIDE
 BANK = 512
 PER_COLUMN = 16
 M_TILES = S2 // P
@@ -50,33 +51,50 @@ def tile_list_impulse_template_scores_kernel(
         p1 = held([P, NP // PER_COLUMN], U16, "p1")
         p2 = held([P, NP // PER_COLUMN], U16, "p2")
 
-        tab_scale_rows = placed([P, T], U8, "tab_scale_rows", 0)
-        w_scale_rows = placed([P, PASSES, H], U8, "w_scale_rows", 8192 - 512)
+        tab_scale_rows = held([P, T], U8, "tab_scale_rows")
+        w_scale_rows = held([P, PASSES, H], U8, "w_scale_rows")
         v_scales_pass1 = held([P, S], U8, "v_scales_pass1")
         tab2_scale_rows = held([P, T3], U8, "tab2_scale_rows")
         for plane in (tab_scale_rows, w_scale_rows, v_scales_pass1, tab2_scale_rows):
             nc.vector.memset(plane[:].bitcast(I32), 0)
 
-        nc.sync.dma_start(idx[:], offs)
-        for q in range(4):
-            nc.gpsimd.dma_start(
-                tab_scale_rows[32 * q : 32 * q + 8, :].bitcast(I32),
-                tab_scales[:, 4 * q : 4 * q + 4, :].bitcast(I32),
+        def load_w1(a):
+            raw = held([P, PACK, H], F32, "w1_raw%d" % a)
+            nc.sync.dma_start(raw[:], w1[512 * a : 512 * (a + 1), :].rearrange("(p j) c -> p j c", j=PACK))
+            return raw
+
+        def load_tab(a):
+            words = held([P, T], U32, "tab%d" % a)
+            nc.sync.dma_start(words[:].bitcast(I32), tab_words[a].rearrange("p t i -> p (t i)").bitcast(I32))
+            return words
+
+        def load_w_scales(first_row, scales, q):
+            nc.sync.dma_start(
+                w_scale_rows[32 * q + first_row : 32 * q + first_row + 4].bitcast(I32),
+                scales[:, 4 * q : 4 * q + 4, :].rearrange("a r n -> r a n").bitcast(I32),
             )
-        w1_raw = [held([P, PACK, H], F32, "w1_raw%d" % a) for a in range(PASSES)]
-        for a in range(PASSES):
-            nc.sync.dma_start(w1_raw[a][:], w1[512 * a : 512 * (a + 1), :].rearrange("(p j) c -> p j c", j=PACK))
+
+        nc.sync.dma_start(idx[:], offs)
+        w1_raw = [load_w1(0)]
+        for r in range(4):
+            nc.sync.dma_start(
+                tab_scale_rows[r:P:16, :].bitcast(I32),
+                tab_scales[:, r:16:4, :].rearrange("a q n -> q a n").bitcast(I32),
+            )
+        w1_raw.append(load_w1(1))
         w3_raw = held([P, PASSES, 2 * H], U8, "w3_raw")
         nc.sync.dma_start(w3_raw[:].bitcast(I32), w3_words.rearrange("a p b -> p a b").bitcast(I32))
-        for first_row, scales in ((0, w3_scales), (4, w2_scales)):
-            for q in range(4):
-                nc.gpsimd.dma_start(
-                    w_scale_rows[32 * q + first_row : 32 * q + first_row + 4].bitcast(I32),
-                    scales[:, 4 * q : 4 * q + 4, :].rearrange("a r n -> r a n").bitcast(I32),
-                )
-        tab = [placed([P, T], U32, "tab%d" % a, 12288 + 16384 * a) for a in range(PASSES)]
-        for a in range(PASSES):
-            nc.sync.dma_start(tab[a][:].bitcast(I32), tab_words[a].rearrange("p t i -> p (t i)").bitcast(I32))
+        for q in range(2):
+            load_w_scales(0, w3_scales, q)
+        tab = [load_tab(0)]
+        for q in range(2, 4):
+            load_w_scales(0, w3_scales, q)
+        for q in range(4):
+            load_w_scales(4, w2_scales, q)
+        v_scales = held([P, S], U8, "v_scales")
+        nc.vector.tensor_copy(v_scales[:], tab_scale_rows[:].indirect(idx[:]))
+        nc.gpsimd.dma_start(v_scales_pass1[0:100, :].bitcast(I32), v_scales[16:116, :].bitcast(I32))
+        tab.append(load_tab(1))
         w2_raw = held([P, PASSES, H], U32, "w2_raw")
         nc.sync.dma_start(w2_raw[:].bitcast(I32), w2_words.rearrange("a p c i -> p a (c i)").bitcast(I32))
         for q in range(4):
@@ -95,13 +113,9 @@ def tile_list_impulse_template_scores_kernel(
         def entries(lst, first, count):
             return lst[:, first // PER_COLUMN : (first + count) // PER_COLUMN]
 
-        v_scales = held([P, S], U8, "v_scales")
-        nc.vector.tensor_copy(v_scales[:], tab_scale_rows[:].indirect(idx[:]))
-        nc.gpsimd.dma_start(v_scales_pass1[0:100, :].bitcast(I32), v_scales[4:104, :].bitcast(I32))
-
         w1_codes = [held([P, H], U32, "w1_codes%d" % a) for a in range(PASSES)]
-        w1_planes = [placed([P, H], U8, "w1_planes%d" % a, H * a) for a in range(PASSES)]
-        w3_codes = placed([P, PASSES, 2 * H], U8, "w3_codes", 2048)
+        w1_planes = [held([P, H], U8, "w1_planes%d" % a) for a in range(PASSES)]
+        w3_codes = held([P, PASSES, 2 * H], U8, "w3_codes")
         for a in range(PASSES):
             grouped = held([P, H * PACK], BF16, "w1_grouped%d" % a)
             nc.scalar.copy(
@@ -113,52 +127,58 @@ def tile_list_impulse_template_scores_kernel(
                 w3_codes[:, a, :].rearrange("p (t m b) -> p t m b", t=PACK, b=2),
                 w3_raw[:, a, :].rearrange("p (m t b) -> p t m b", t=PACK, b=2),
             )
-        w_planes = placed([P, PASSES, H], U8, "w_planes", 1024)
-        nc.vector.tensor_copy(
-            w_planes[:].rearrange("p a (t m) -> p a t m", t=PACK),
-            w_scale_rows[:].rearrange("p a (m t) -> p a t m", t=PACK),
-        )
 
-        v_words = [placed([P, PASSES * BANK], U32, "v_words%d" % half, 4096 + 4096 * half) for half in range(2)]
-        for a in range(PASSES):
+        v_words = [placed([P, PASSES * BANK], U32, "v_words%d" % half, 4096 * half) for half in range(2)]
+
+        def gather_windows(a):
             for half in range(2):
                 nc.vector.tensor_copy(
                     v_words[half][:, a * BANK : (a + 1) * BANK], tab[a][:].indirect(entries(idx, half * BANK, BANK))
                 )
-        w2_codes = placed([P, PASSES, H], U32, "w2_codes", 12288)
+
+        gather_windows(0)
+        w_planes = held([P, PASSES, H], U8, "w_planes")
+        nc.vector.tensor_copy(
+            w_planes[:].rearrange("p a (t m) -> p a t m", t=PACK),
+            w_scale_rows[:].rearrange("p a (m t) -> p a t m", t=PACK),
+        )
+        gather_windows(1)
+        w2_codes = held([P, PASSES, H], U32, "w2_codes")
         nc.vector.tensor_copy(
             w2_codes[:].rearrange("p a (t m) -> p a t m", t=PACK),
             w2_raw[:].rearrange("p a (m t) -> p a t m", t=PACK),
         )
 
-        def one_pass(bank, a, unit, stationary, moving_planes):
-            cols = slice(unit * UNIT, (unit + 1) * UNIT)
-            half, first = divmod(unit * UNIT, BANK)
-            for t in range(PACK):
+        v_planes = (v_scales, v_scales_pass1)
+
+        def one_pass(bank, a, stationary, slots, first, width):
+            half, at = divmod(first, BANK)
+            for i, t in enumerate(slots):
                 codes, plane = stationary(a, t)
                 nc.tensor.matmul_mx(
-                    out=bank[:, t, :],
+                    out=bank[:, i, :],
                     lhsT=codes,
                     lhsT_scale=plane,
-                    rhs=v_words[half][:, a * BANK + first : a * BANK + first + UNIT].bitcast(FP8X4),
-                    rhs_scale=moving_planes[a][:, cols],
-                    start=(a == 0 and t == 0),
-                    stop=(a == PASSES - 1 and t == PACK - 1),
+                    rhs=v_words[half][:, a * BANK + at : a * BANK + at + width].bitcast(FP8X4),
+                    rhs_scale=v_planes[a][:, first : first + width],
+                    start=(a == 0 and i == 0),
+                    stop=(a == PASSES - 1 and i == len(slots) - 1),
                 )
 
         opened = {}
 
-        def begin(tag, bufs, unit, stationary, moving_planes):
-            bank = psum.tile([P, PACK, UNIT], F32, name=tag, tag=tag, bufs=bufs)
-            one_pass(bank, 0, unit, stationary, moving_planes)
-            opened[tag, unit] = bank
+        def begin(tag, bufs, stationary, slots, first):
+            width = BANK // len(slots)
+            bank = psum.tile([P, len(slots), width], F32, name=tag, tag=tag, bufs=bufs)
+            one_pass(bank, 0, stationary, slots, first, width)
+            opened[tag, slots, first] = bank
 
-        def product(tag, bufs, unit, stationary, moving_planes):
-            if (tag, unit) not in opened:
-                begin(tag, bufs, unit, stationary, moving_planes)
-            bank = opened[tag, unit]
-            one_pass(bank, 1, unit, stationary, moving_planes)
-            return bank[:].rearrange("p t j -> p j t")
+        def product(tag, bufs, stationary, slots, first):
+            if (tag, slots, first) not in opened:
+                begin(tag, bufs, stationary, slots, first)
+            bank = opened[tag, slots, first]
+            one_pass(bank, 1, stationary, slots, first, BANK // len(slots))
+            return bank
 
         def w1_tile(a, t):
             return w1_codes[a][:, P * t : P * (t + 1)].bitcast(FP8X4), w1_planes[a][:, P * t : P * (t + 1)]
@@ -169,9 +189,6 @@ def tile_list_impulse_template_scores_kernel(
         def w3_tile(a, t):
             return w3_codes[:, a, 2 * P * t : 2 * P * (t + 1)].bitcast(FP4X4), w_planes[:, a, P * t : P * (t + 1)]
 
-        packed_planes = (v_scales[:], v_scales[4:P, :])
-        apart_planes = (v_scales[:], v_scales_pass1[:])
-
         h_codes = held([P, S], U32, "h_codes")
         h_plane = held([P, S], U8, "h_plane")
         v2_words = {}
@@ -179,8 +196,8 @@ def tile_list_impulse_template_scores_kernel(
         scores = [held([P, S], F32, "scores%d" % m) for m in range(M_TILES)]
 
         def gather_templates(half):
-            v2_plane[half] = placed([P, 256], U8, "v2_plane%d" % half, 4096 + 4096 * half + 1024)
-            v2_words[half] = placed([P, 256], U32, "v2_words%d" % half, 4096 + 4096 * half)
+            v2_plane[half] = placed([P, 256], U8, "v2_plane%d" % half, 4096 * half + 1024)
+            v2_words[half] = placed([P, 256], U32, "v2_words%d" % half, 4096 * half)
             nc.vector.tensor_copy(v2_plane[half][:], tab2_scale_rows[:].indirect(entries(idx2, 256 * half, 256)))
             nc.vector.tensor_copy(v2_words[half][:], tab2[:].indirect(entries(idx2, 256 * half, 256)))
 
@@ -205,38 +222,61 @@ def tile_list_impulse_template_scores_kernel(
         def interleaved(tile):
             return tile[:].rearrange("p (j t) -> p j t", t=PACK)
 
+        pairs = ((0, 1), (2, 3))
+        quad = (0, 1, 2, 3)
+        begin("z1", 3, w1_tile, pairs[0], 0)
+        begin("z1", 3, w1_tile, pairs[1], 0)
+        begin("z1", 3, w1_tile, pairs[0], WIDE)
         for unit in range(3):
-            begin("z1", 3, unit, w1_tile, packed_planes)
-        for unit in range(3):
-            begin("z3", 3, unit, w3_tile, apart_planes)
+            begin("z3", 3, w3_tile, quad, unit * UNIT)
         shapes = {}
-        for step in range(UNITS + 1):
-            if step < UNITS:
-                z1 = product("z1", 3, step, w1_tile, packed_planes)
-                z2 = product("z2", 2, step, w2_tile, packed_planes)
-                inner = ring.tile([P, BANK], F32, name="inner")
-                nc.scalar.activation(interleaved(inner), z1, TANH)
+        for step in range(STEPS + 1):
+            if step < STEPS:
+                sums = []
+                for pair in pairs:
+                    z1 = product("z1", 3, w1_tile, pair, step * WIDE)
+                    z2 = product("z2", 2, w2_tile, pair, step * WIDE)
+                    inner = ring.tile([P, 2, WIDE], F32, name="inner")
+                    nc.scalar.activation(inner[:], z1[:], TANH)
+                    sums.append((z2, inner))
             if step >= 1:
-                z3 = product("z3", 3, step - 1, w3_tile, apart_planes)
-                h = ring.tile([P, BANK], BF16, name="h", align_bytes=64)
-                nc.vector.tensor_tensor(interleaved(h), z3, interleaved(shapes[step - 1]), MULT)
-            if step < UNITS:
-                total = ring.tile([P, BANK], F32, name="total")
-                nc.vector.tensor_tensor(interleaved(total), z2, interleaved(inner), ADD)
-                shape = ring.tile([P, BANK], F32, name="shape")
-                nc.scalar.activation(shape[:], total[:], TANH)
-                shapes[step] = shape
-            if step >= 1:
-                cols = slice((step - 1) * UNIT, step * UNIT)
-                nc.vector.quantize_mx(out=h_codes[:, cols].bitcast(FP8X4), scales=h_plane[:, cols], in_=h[:])
-            if step == 4:
+                h = ring.tile([P, 2, BANK], BF16, name="h", align_bytes=64)
+                for x in range(2):
+                    unit = 2 * (step - 1) + x
+                    z3 = product("z3", 3, w3_tile, quad, unit * UNIT)
+                    nc.vector.tensor_tensor(
+                        h[:, x, :].rearrange("p (j t) -> p j t", t=PACK),
+                        z3[:].rearrange("p t j -> p j t"),
+                        interleaved(shapes[unit]),
+                        MULT,
+                    )
+            if step < STEPS:
+                total = ring.tile([P, PACK, WIDE], F32, name="total", bufs=2)
+                for c, (z2, inner) in enumerate(sums):
+                    nc.vector.tensor_tensor(total[:, 2 * c : 2 * c + 2, :], z2[:], inner[:], ADD)
+                for x in range(2):
+                    shape = ring.tile([P, BANK], F32, name="shape", bufs=4)
+                    nc.scalar.activation(
+                        shape[:].rearrange("p (c i t) -> p c t i", i=PACK, t=PACK),
+                        total[:, :, x * UNIT : (x + 1) * UNIT].rearrange("p t (c i) -> p c t i", i=PACK),
+                        TANH,
+                    )
+                    shapes[2 * step + x] = shape
+            if 1 <= step < STEPS:
+                cols = slice((step - 1) * WIDE, step * WIDE)
+                nc.vector.quantize_mx(
+                    out=h_codes[:, cols].bitcast(FP8X4), scales=h_plane[:, cols], in_=h[:].rearrange("p x c -> p (x c)")
+                )
+            if step == 2:
                 gather_templates(0)
-            if step == 5:
+            if step == 3:
                 score(0, 0, [BANK])
                 score(1, 0, [BANK])
-            if step == 7:
-                score(0, BANK, [256, 128])
-        score(0, S - UNIT, [UNIT])
+        for x in range(2):
+            cols = slice(S - WIDE + x * UNIT, S - WIDE + (x + 1) * UNIT)
+            nc.vector.quantize_mx(out=h_codes[:, cols].bitcast(FP8X4), scales=h_plane[:, cols], in_=h[:, x, :])
+        score(0, BANK, [WIDE])
+        score(0, S - WIDE, [UNIT, UNIT])
         gather_templates(1)
         score(1, BANK, [BANK])
 
@@ -247,10 +287,11 @@ def tile_list_impulse_template_scores_kernel(
             nc.scalar.activation(bound[:], scaled[:], TANH)
             return bound
 
-        def finish(m, bound):
-            result = ring.tile([P, NP], F32, name="result")
-            nc.vector.tensor_tensor(result[:], scores[m][:].indirect(p1[:]), bound[:], SUB)
-            nc.sync.dma_start(out[P * m : P * (m + 1), :], result[:])
+        def finish(m, bound, first, count):
+            result = ring.tile([P, count], F32, name="result")
+            cols = slice(first, first + count)
+            nc.vector.tensor_tensor(result[:], scores[m][:].indirect(entries(p1, first, count)), bound[:, cols], SUB)
+            nc.sync.dma_start(out[P * m : P * (m + 1), cols], result[:])
 
         bounds = {0: bounded(0)}
         for m in range(M_TILES):
@@ -259,4 +300,8 @@ def tile_list_impulse_template_scores_kernel(
             if m + 2 < M_TILES:
                 score(m + 2, 0, [BANK])
                 score(m + 2, BANK, [BANK])
-            finish(m, bounds[m])
+            if m + 1 < M_TILES:
+                finish(m, bounds[m], 0, NP)
+            else:
+                finish(m, bounds[m], 0, NP // 2)
+                finish(m, bounds[m], NP // 2, NP // 2)

@@ -52,10 +52,11 @@ def tile_list_impulse_template_scores_kernel(
         p2 = held([P, NP // PER_COLUMN], U16, "p2")
 
         tab_scale_rows = held([P, T], U8, "tab_scale_rows")
-        w_scale_rows = held([P, PASSES, H], U8, "w_scale_rows")
+        w2_scale_rows = held([P, PASSES, H], U8, "w2_scale_rows")
+        w3_scale_rows = held([P, PASSES, H], U8, "w3_scale_rows")
         v_scales_pass1 = held([P, S], U8, "v_scales_pass1")
         tab2_scale_rows = held([P, T3], U8, "tab2_scale_rows")
-        for plane in (tab_scale_rows, w_scale_rows, v_scales_pass1, tab2_scale_rows):
+        for plane in (tab_scale_rows, w2_scale_rows, w3_scale_rows, v_scales_pass1, tab2_scale_rows):
             nc.vector.memset(plane[:].bitcast(I32), 0)
 
         def load_w1(a):
@@ -64,15 +65,16 @@ def tile_list_impulse_template_scores_kernel(
             return raw
 
         def load_tab(a):
-            words = held([P, T], U32, "tab%d" % a)
+            words = placed([P, T], U32, "tab%d" % a, 8192 + 16384 * a)
             nc.sync.dma_start(words[:].bitcast(I32), tab_words[a].rearrange("p t i -> p (t i)").bitcast(I32))
             return words
 
-        def load_w_scales(first_row, scales, q):
-            nc.sync.dma_start(
-                w_scale_rows[32 * q + first_row : 32 * q + first_row + 4].bitcast(I32),
-                scales[:, 4 * q : 4 * q + 4, :].rearrange("a r n -> r a n").bitcast(I32),
-            )
+        def load_w_scales(rows, scales):
+            for q in range(4):
+                nc.sync.dma_start(
+                    rows[32 * q : 32 * q + 4].bitcast(I32),
+                    scales[:, 4 * q : 4 * q + 4, :].rearrange("a r n -> r a n").bitcast(I32),
+                )
 
         nc.sync.dma_start(idx[:], offs)
         w1_raw = [load_w1(0)]
@@ -82,21 +84,17 @@ def tile_list_impulse_template_scores_kernel(
                 tab_scales[:, r:16:4, :].rearrange("a q n -> q a n").bitcast(I32),
             )
         w1_raw.append(load_w1(1))
-        w3_raw = held([P, PASSES, 2 * H], U8, "w3_raw")
-        nc.sync.dma_start(w3_raw[:].bitcast(I32), w3_words.rearrange("a p b -> p a b").bitcast(I32))
-        for q in range(2):
-            load_w_scales(0, w3_scales, q)
         tab = [load_tab(0)]
-        for q in range(2, 4):
-            load_w_scales(0, w3_scales, q)
-        for q in range(4):
-            load_w_scales(4, w2_scales, q)
         v_scales = held([P, S], U8, "v_scales")
         nc.vector.tensor_copy(v_scales[:], tab_scale_rows[:].indirect(idx[:]))
         nc.gpsimd.dma_start(v_scales_pass1[0:100, :].bitcast(I32), v_scales[16:116, :].bitcast(I32))
         tab.append(load_tab(1))
         w2_raw = held([P, PASSES, H], U32, "w2_raw")
         nc.sync.dma_start(w2_raw[:].bitcast(I32), w2_words.rearrange("a p c i -> p a (c i)").bitcast(I32))
+        load_w_scales(w2_scale_rows, w2_scales)
+        w3_raw = held([P, PASSES, 2 * H], U8, "w3_raw")
+        nc.sync.dma_start(w3_raw[:].bitcast(I32), w3_words.rearrange("a p b -> p a b").bitcast(I32))
+        load_w_scales(w3_scale_rows, w3_scales)
         for q in range(4):
             nc.sync.dma_start(
                 tab2_scale_rows[32 * q : 32 * q + 4, :].bitcast(I32),
@@ -115,7 +113,6 @@ def tile_list_impulse_template_scores_kernel(
 
         w1_codes = [held([P, H], U32, "w1_codes%d" % a) for a in range(PASSES)]
         w1_planes = [held([P, H], U8, "w1_planes%d" % a) for a in range(PASSES)]
-        w3_codes = held([P, PASSES, 2 * H], U8, "w3_codes")
         for a in range(PASSES):
             grouped = held([P, H * PACK], BF16, "w1_grouped%d" % a)
             nc.scalar.copy(
@@ -123,10 +120,6 @@ def tile_list_impulse_template_scores_kernel(
                 w1_raw[a][:].rearrange("p j (m t) -> p m t j", t=PACK),
             )
             nc.vector.quantize_mx(out=w1_codes[a][:].bitcast(FP8X4), scales=w1_planes[a][:], in_=grouped[:])
-            nc.vector.tensor_copy(
-                w3_codes[:, a, :].rearrange("p (t m b) -> p t m b", t=PACK, b=2),
-                w3_raw[:, a, :].rearrange("p (m t b) -> p t m b", t=PACK, b=2),
-            )
 
         v_words = [placed([P, PASSES * BANK], U32, "v_words%d" % half, 4096 * half) for half in range(2)]
 
@@ -137,17 +130,20 @@ def tile_list_impulse_template_scores_kernel(
                 )
 
         gather_windows(0)
-        w_planes = held([P, PASSES, H], U8, "w_planes")
-        nc.vector.tensor_copy(
-            w_planes[:].rearrange("p a (t m) -> p a t m", t=PACK),
-            w_scale_rows[:].rearrange("p a (m t) -> p a t m", t=PACK),
-        )
         gather_windows(1)
-        w2_codes = held([P, PASSES, H], U32, "w2_codes")
-        nc.vector.tensor_copy(
-            w2_codes[:].rearrange("p a (t m) -> p a t m", t=PACK),
-            w2_raw[:].rearrange("p a (m t) -> p a t m", t=PACK),
-        )
+
+        def dealt(raw, dtype, view, name, at):
+            tile = placed(list(raw.shape), dtype, name, 8192 + 16384 + at)
+            nc.vector.tensor_copy(
+                tile[:].bitcast(view).rearrange("p a (t m) -> p a t m", t=PACK),
+                raw[:].bitcast(view).rearrange("p a (m t) -> p a t m", t=PACK),
+            )
+            return tile
+
+        w2_codes = dealt(w2_raw, U32, U32, "w2_codes", 0)
+        w2_planes = dealt(w2_scale_rows, U8, U8, "w2_planes", 4096)
+        w3_codes = dealt(w3_raw, U8, U16, "w3_codes", 5120)
+        w3_planes = dealt(w3_scale_rows, U8, U8, "w3_planes", 7168)
 
         v_planes = (v_scales, v_scales_pass1)
 
@@ -167,9 +163,9 @@ def tile_list_impulse_template_scores_kernel(
 
         opened = {}
 
-        def begin(tag, bufs, stationary, slots, first):
+        def begin(tag, bufs, stationary, slots, first, home=None):
             width = BANK // len(slots)
-            bank = psum.tile([P, len(slots), width], F32, name=tag, tag=tag, bufs=bufs)
+            bank = psum.tile([P, len(slots), width], F32, name=home or tag, tag=home or tag, bufs=bufs)
             one_pass(bank, 0, stationary, slots, first, width)
             opened[tag, slots, first] = bank
 
@@ -184,10 +180,10 @@ def tile_list_impulse_template_scores_kernel(
             return w1_codes[a][:, P * t : P * (t + 1)].bitcast(FP8X4), w1_planes[a][:, P * t : P * (t + 1)]
 
         def w2_tile(a, t):
-            return w2_codes[:, a, P * t : P * (t + 1)].bitcast(FP8X4), w_planes[4:P, a, P * t : P * (t + 1)]
+            return w2_codes[:, a, P * t : P * (t + 1)].bitcast(FP8X4), w2_planes[:, a, P * t : P * (t + 1)]
 
         def w3_tile(a, t):
-            return w3_codes[:, a, 2 * P * t : 2 * P * (t + 1)].bitcast(FP4X4), w_planes[:, a, P * t : P * (t + 1)]
+            return w3_codes[:, a, 2 * P * t : 2 * P * (t + 1)].bitcast(FP4X4), w3_planes[:, a, P * t : P * (t + 1)]
 
         h_codes = held([P, S], U32, "h_codes")
         h_plane = held([P, S], U8, "h_plane")
@@ -224,21 +220,25 @@ def tile_list_impulse_template_scores_kernel(
 
         pairs = ((0, 1), (2, 3))
         quad = (0, 1, 2, 3)
-        begin("z1", 3, w1_tile, pairs[0], 0)
-        begin("z1", 3, w1_tile, pairs[1], 0)
-        begin("z1", 3, w1_tile, pairs[0], WIDE)
-        for unit in range(3):
-            begin("z3", 3, w3_tile, quad, unit * UNIT)
+        homes = ["z2"] * 2 + ["z3"] * 3 + ["z1"] * 3
+        for step in range(STEPS):
+            for c, pair in enumerate(pairs):
+                home = homes[2 * step + c]
+                begin("z1", 2 if home == "z2" else 3, w1_tile, pair, step * WIDE, home)
+        inners = {}
+
+        def first_tanh(step):
+            for pair in pairs:
+                z1 = product("z1", 3, w1_tile, pair, step * WIDE)
+                inners[step, pair] = ring.tile([P, 2, WIDE], F32, name="inner", bufs=4)
+                nc.scalar.activation(inners[step, pair][:], z1[:], TANH)
+
+        first_tanh(0)
+        first_tanh(1)
         shapes = {}
         for step in range(STEPS + 1):
             if step < STEPS:
-                sums = []
-                for pair in pairs:
-                    z1 = product("z1", 3, w1_tile, pair, step * WIDE)
-                    z2 = product("z2", 2, w2_tile, pair, step * WIDE)
-                    inner = ring.tile([P, 2, WIDE], F32, name="inner")
-                    nc.scalar.activation(inner[:], z1[:], TANH)
-                    sums.append((z2, inner))
+                sums = [(product("z2", 2, w2_tile, pair, step * WIDE), inners[step, pair]) for pair in pairs]
             if step >= 1:
                 h = ring.tile([P, 2, BANK], BF16, name="h", align_bytes=64)
                 for x in range(2):
@@ -262,6 +262,8 @@ def tile_list_impulse_template_scores_kernel(
                         TANH,
                     )
                     shapes[2 * step + x] = shape
+                if step + 2 < STEPS:
+                    first_tanh(step + 2)
             if 1 <= step < STEPS:
                 cols = slice((step - 1) * WIDE, step * WIDE)
                 nc.vector.quantize_mx(

@@ -116,8 +116,8 @@ def tile_list_impulse_template_scores_kernel(
         for a in range(PASSES):
             grouped = held([P, H * PACK], BF16, "w1_grouped%d" % a)
             nc.scalar.copy(
-                grouped[:].rearrange("p (t m j) -> p m t j", t=PACK, j=PACK),
-                w1_raw[a][:].rearrange("p j (m t) -> p m t j", t=PACK),
+                grouped[:].rearrange("p (t m j) -> p t m j", t=PACK, j=PACK),
+                w1_raw[a][:].rearrange("p j (m t) -> p t m j", t=PACK),
             )
             nc.vector.quantize_mx(out=w1_codes[a][:].bitcast(FP8X4), scales=w1_planes[a][:], in_=grouped[:])
 
@@ -257,8 +257,8 @@ def tile_list_impulse_template_scores_kernel(
                 for x in range(2):
                     shape = ring.tile([P, BANK], F32, name="shape", bufs=4)
                     nc.scalar.activation(
-                        shape[:].rearrange("p (c i t) -> p c t i", i=PACK, t=PACK),
-                        total[:, :, x * UNIT : (x + 1) * UNIT].rearrange("p t (c i) -> p c t i", i=PACK),
+                        interleaved(shape),
+                        total[:, :, x * UNIT : (x + 1) * UNIT].rearrange("p t j -> p j t"),
                         TANH,
                     )
                     shapes[2 * step + x] = shape

from contextlib import ExitStack

import concourse.mybir as mybir

K, T, S, H, T3, S2, NP = 1024, 4096, 1024, 512, 2048, 512, 512
FLOPS = 2 * (3 * K * H * S + H * S2 * S)

F32 = mybir.dt.float32
BF16 = mybir.dt.bfloat16
I32 = mybir.dt.int32
U32 = mybir.dt.uint32
U16 = mybir.dt.uint16
U8 = mybir.dt.uint8
FP8X4 = mybir.dt.float8_e4m3fn_x4
FP4X4 = mybir.dt.float4_e2m1fn_x4
TANH = mybir.ActivationFunctionType.Tanh
ADD = mybir.AluOpType.add
MULT = mybir.AluOpType.mult
SUB = mybir.AluOpType.subtract

P = 128
PACK = 4
PASSES = K // (P * PACK)
UNIT = 128
WIDE = 256
STEPS = S // WIDE
BANK = 512
PER_COLUMN = 16
M_TILES = S2 // P


def tile_list_impulse_template_scores_kernel(
    tc, tab_words, tab_scales, offs, w1, w2_words, w2_scales, w3_words, w3_scales,
    tab2_words, tab2_scales, offs2, pos1, pos2, rel, out,
):
    nc = tc.nc
    with ExitStack() as ctx:
        keep = ctx.enter_context(tc.tile_pool(name="keep", bufs=1))
        reused = ctx.enter_context(tc.tile_pool(name="reused", bufs=1))
        ring = ctx.enter_context(tc.tile_pool(name="ring", bufs=3))
        psum = ctx.enter_context(tc.psum_pool(name="psum", bufs=1))

        def held(shape, dtype, name):
            return keep.tile(shape, dtype, name=name, align_bytes=64)

        def placed(shape, dtype, name, offset):
            return reused.tile(shape, dtype, name=name, align_bytes=64, offset=offset)

        idx = held([P, S // PER_COLUMN], U16, "idx")
        idx2 = held([P, S2 // PER_COLUMN], U16, "idx2")
        p1 = held([P, NP // PER_COLUMN], U16, "p1")
        p2 = held([P, NP // PER_COLUMN], U16, "p2")

        tab_scale_rows = held([P, T], U8, "tab_scale_rows")
        w2_scale_rows = held([P, PASSES, H], U8, "w2_scale_rows")
        w3_scale_rows = held([P, PASSES, H], U8, "w3_scale_rows")
        v_scales_pass1 = held([P, S], U8, "v_scales_pass1")
        tab2_scale_rows = held([P, T3], U8, "tab2_scale_rows")
        for plane in (tab_scale_rows, w2_scale_rows, w3_scale_rows, v_scales_pass1, tab2_scale_rows):
            nc.vector.memset(plane[:].bitcast(I32), 0)

        def load_w1(a):
            raw = held([P, PACK, H], F32, "w1_raw%d" % a)
            nc.sync.dma_start(raw[:], w1[512 * a : 512 * (a + 1), :].rearrange("(p j) c -> p j c", j=PACK))
            return raw

        def load_tab(a):
            words = placed([P, T], U32, "tab%d" % a, 8192 + 16384 * a)
            nc.sync.dma_start(words[:].bitcast(I32), tab_words[a].rearrange("p t i -> p (t i)").bitcast(I32))
            return words

        def load_w_scales(rows, scales):
            for q in range(4):
                nc.sync.dma_start(
                    rows[32 * q : 32 * q + 4].bitcast(I32),
                    scales[:, 4 * q : 4 * q + 4, :].rearrange("a r n -> r a n").bitcast(I32),
                )

        nc.sync.dma_start(idx[:], offs)
        w1_raw = [load_w1(0)]
        for r in range(4):
            nc.sync.dma_start(
                tab_scale_rows[r:P:16, :].bitcast(I32),
                tab_scales[:, r:16:4, :].rearrange("a q n -> q a n").bitcast(I32),
            )
        w1_raw.append(load_w1(1))
        tab = [load_tab(0)]
        v_scales = held([P, S], U8, "v_scales")
        nc.vector.tensor_copy(v_scales[:], tab_scale_rows[:].indirect(idx[:]))
        nc.gpsimd.dma_start(v_scales_pass1[0:100, :].bitcast(I32), v_scales[16:116, :].bitcast(I32))
        tab.append(load_tab(1))
        w2_raw = held([P, PASSES, H], U32, "w2_raw")
        nc.sync.dma_start(w2_raw[:].bitcast(I32), w2_words.rearrange("a p c i -> p a (c i)").bitcast(I32))
        load_w_scales(w2_scale_rows, w2_scales)
        w3_raw = held([P, PASSES, 2 * H], U8, "w3_raw")
        nc.sync.dma_start(w3_raw[:].bitcast(I32), w3_words.rearrange("a p b -> p a b").bitcast(I32))
        load_w_scales(w3_scale_rows, w3_scales)
        for q in range(4):
            nc.sync.dma_start(
                tab2_scale_rows[32 * q : 32 * q + 4, :].bitcast(I32),
                tab2_scales[0, 4 * q : 4 * q + 4, :].bitcast(I32),
            )
        tab2 = held([P, T3], U32, "tab2")
        nc.sync.dma_start(tab2[:].bitcast(I32), tab2_words[0].rearrange("p t i -> p (t i)").bitcast(I32))
        nc.sync.dma_start(idx2[:], offs2)
        rel_rows = held([P, M_TILES, NP], F32, "rel_rows")
        nc.sync.dma_start(rel_rows[:], rel.rearrange("(m p) n -> p m n", p=P))
        nc.sync.dma_start(p2[:], pos2)
        nc.sync.dma_start(p1[:], pos1)

        def entries(lst, first, count):
            return lst[:, first // PER_COLUMN : (first + count) // PER_COLUMN]

        w1_codes = [held([P, H], U32, "w1_codes%d" % a) for a in range(PASSES)]
        w1_planes = [held([P, H], U8, "w1_planes%d" % a) for a in range(PASSES)]
        for a in range(PASSES):
            grouped = held([P, H * PACK], BF16, "w1_grouped%d" % a)
            nc.scalar.copy(
                grouped[:].rearrange("p (t m j) -> p t m j", t=PACK, j=PACK),
                w1_raw[a][:].rearrange("p j (m t) -> p t m j", t=PACK),
            )
            nc.vector.quantize_mx(out=w1_codes[a][:].bitcast(FP8X4), scales=w1_planes[a][:], in_=grouped[:])

        v_words = [placed([P, PASSES * BANK], U32, "v_words%d" % half, 4096 * half) for half in range(2)]

        def gather_windows(a):
            for half in range(2):
                nc.vector.tensor_copy(
                    v_words[half][:, a * BANK : (a + 1) * BANK], tab[a][:].indirect(entries(idx, half * BANK, BANK))
                )

        gather_windows(0)
        gather_windows(1)

        def dealt(raw, dtype, view, name, at):
            tile = placed(list(raw.shape), dtype, name, 8192 + 16384 + at)
            nc.vector.tensor_copy(
                tile[:].bitcast(view).rearrange("p a (t m) -> p a t m", t=PACK),
                raw[:].bitcast(view).rearrange("p a (m t) -> p a t m", t=PACK),
            )
            return tile

        w2_codes = dealt(w2_raw, U32, U32, "w2_codes", 0)
        w2_planes = dealt(w2_scale_rows, U8, U8, "w2_planes", 4096)
        w3_codes = dealt(w3_raw, U8, U16, "w3_codes", 5120)
        w3_planes = dealt(w3_scale_rows, U8, U8, "w3_planes", 7168)

        v_planes = (v_scales, v_scales_pass1)

        def one_pass(bank, a, stationary, slots, first, width):
            half, at = divmod(first, BANK)
            for i, t in enumerate(slots):
                codes, plane = stationary(a, t)
                nc.tensor.matmul_mx(
                    out=bank[:, i, :],
                    lhsT=codes,
                    lhsT_scale=plane,
                    rhs=v_words[half][:, a * BANK + at : a * BANK + at + width].bitcast(FP8X4),
                    rhs_scale=v_planes[a][:, first : first + width],
                    start=(a == 0 and i == 0),
                    stop=(a == PASSES - 1 and i == len(slots) - 1),
                )

        opened = {}

        def begin(tag, bufs, stationary, slots, first, home=None):
            width = BANK // len(slots)
            bank = psum.tile([P, len(slots), width], F32, name=home or tag, tag=home or tag, bufs=bufs)
            one_pass(bank, 0, stationary, slots, first, width)
            opened[tag, slots, first] = bank

        def product(tag, bufs, stationary, slots, first):
            if (tag, slots, first) not in opened:
                begin(tag, bufs, stationary, slots, first)
            bank = opened[tag, slots, first]
            one_pass(bank, 1, stationary, slots, first, BANK // len(slots))
            return bank

        def w1_tile(a, t):
            return w1_codes[a][:, P * t : P * (t + 1)].bitcast(FP8X4), w1_planes[a][:, P * t : P * (t + 1)]

        def w2_tile(a, t):
            return w2_codes[:, a, P * t : P * (t + 1)].bitcast(FP8X4), w2_planes[:, a, P * t : P * (t + 1)]

        def w3_tile(a, t):
            return w3_codes[:, a, 2 * P * t : 2 * P * (t + 1)].bitcast(FP4X4), w3_planes[:, a, P * t : P * (t + 1)]

        h_codes = held([P, S], U32, "h_codes")
        h_plane = held([P, S], U8, "h_plane")
        v2_words = {}
        v2_plane = {}
        scores = [held([P, S], F32, "scores%d" % m) for m in range(M_TILES)]

        def gather_templates(half):
            v2_plane[half] = placed([P, 256], U8, "v2_plane%d" % half, 4096 * half + 1024)
            v2_words[half] = placed([P, 256], U32, "v2_words%d" % half, 4096 * half)
            nc.vector.tensor_copy(v2_plane[half][:], tab2_scale_rows[:].indirect(entries(idx2, 256 * half, 256)))
            nc.vector.tensor_copy(v2_words[half][:], tab2[:].indirect(entries(idx2, 256 * half, 256)))

        def score(m, first, widths):
            bank = psum.tile([P, BANK], F32, name="z1", tag="z1", bufs=3)
            rows = slice(P * (m % 2), P * (m % 2 + 1))
            at = 0
            for width in widths:
                cols = slice(first + at, first + at + width)
                nc.tensor.matmul_mx(
                    out=bank[:, at : at + width],
                    lhsT=v2_words[m // 2][:, rows].bitcast(FP8X4),
                    lhsT_scale=v2_plane[m // 2][:, rows],
                    rhs=h_codes[:, cols].bitcast(FP8X4),
                    rhs_scale=h_plane[:, cols],
                    start=True,
                    stop=True,
                )
                at = at + width
            nc.scalar.copy(scores[m][:, first : first + at], bank[:, 0:at])

        def interleaved(tile):
            return tile[:].rearrange("p (j t) -> p j t", t=PACK)

        pairs = ((0, 1), (2, 3))
        quad = (0, 1, 2, 3)
        homes = ["z2"] * 2 + ["z3"] * 3 + ["z1"] * 3
        for step in range(STEPS):
            for c, pair in enumerate(pairs):
                home = homes[2 * step + c]
                begin("z1", 2 if home == "z2" else 3, w1_tile, pair, step * WIDE, home)
        inners = {}

        def first_tanh(step):
            for pair in pairs:
                z1 = product("z1", 3, w1_tile, pair, step * WIDE)
                inners[step, pair] = ring.tile([P, 2, WIDE], F32, name="inner", bufs=4)
                nc.scalar.activation(inners[step, pair][:], z1[:], TANH)

        first_tanh(0)
        first_tanh(1)
        shapes = {}
        for step in range(STEPS + 1):
            if step < STEPS:
                sums = [(product("z2", 2, w2_tile, pair, step * WIDE), inners[step, pair]) for pair in pairs]
            if step >= 1:
                h = ring.tile([P, 2, BANK], BF16, name="h", align_bytes=64)
                for x in range(2):
                    unit = 2 * (step - 1) + x
                    z3 = product("z3", 3, w3_tile, quad, unit * UNIT)
                    nc.vector.tensor_tensor(
                        h[:, x, :].rearrange("p (j t) -> p j t", t=PACK),
                        z3[:].rearrange("p t j -> p j t"),
                        interleaved(shapes[unit]),
                        MULT,
                    )
            if step < STEPS:
                total = ring.tile([P, PACK, WIDE], F32, name="total", bufs=2)
                for c, (z2, inner) in enumerate(sums):
                    nc.vector.tensor_tensor(total[:, 2 * c : 2 * c + 2, :], z2[:], inner[:], ADD)
                for x in range(2):
                    shape = ring.tile([P, BANK], F32, name="shape", bufs=4)
                    nc.scalar.activation(
                        interleaved(shape),
                        total[:, :, x * UNIT : (x + 1) * UNIT].rearrange("p t j -> p j t"),
                        TANH,
                    )
                    shapes[2 * step + x] = shape
                if step + 2 < STEPS:
                    first_tanh(step + 2)
            if 1 <= step < STEPS:
                cols = slice((step - 1) * WIDE, step * WIDE)
                nc.vector.quantize_mx(
                    out=h_codes[:, cols].bitcast(FP8X4), scales=h_plane[:, cols], in_=h[:].rearrange("p x c -> p (x c)")
                )
            if step == 2:
                gather_templates(0)
            if step == 3:
                score(0, 0, [BANK])
                score(1, 0, [BANK])
        for x in range(2):
            cols = slice(S - WIDE + x * UNIT, S - WIDE + (x + 1) * UNIT)
            nc.vector.quantize_mx(out=h_codes[:, cols].bitcast(FP8X4), scales=h_plane[:, cols], in_=h[:, x, :])
        score(0, BANK, [WIDE])
        score(0, S - WIDE, [UNIT, UNIT])
        gather_templates(1)
        score(1, BANK, [BANK])

        def bounded(m):
            scaled = ring.tile([P, NP], F32, name="scaled")
            nc.vector.tensor_tensor(scaled[:], scores[m][:].indirect(p2[:]), rel_rows[:, m, :], MULT)
            bound = ring.tile([P, NP], F32, name="bound")
            nc.scalar.activation(bound[:], scaled[:], TANH)
            return bound

        def finish(m, bound, first, count):
            result = ring.tile([P, count], F32, name="result")
            cols = slice(first, first + count)
            nc.vector.tensor_tensor(result[:], scores[m][:].indirect(entries(p1, first, count)), bound[:, cols], SUB)
            nc.sync.dma_start(out[P * m : P * (m + 1), cols], result[:])

        bounds = {0: bounded(0)}
        for m in range(M_TILES):
            if m + 1 < M_TILES:
                bounds[m + 1] = bounded(m + 1)
            if m + 2 < M_TILES:
                score(m + 2, 0, [BANK])
                score(m + 2, BANK, [BANK])
            if m + 1 < M_TILES:
                finish(m, bounds[m], 0, NP)
            else:
                finish(m, bounds[m], 0, NP // 2)
                finish(m, bounds[m], NP // 2, NP // 2)
